import numpy as np
import ml_dtypes


def mxq(x, axis, fmt="e4m3"):
    dtype, down = {"e4m3": (ml_dtypes.float8_e4m3fn, 7), "e5m2": (ml_dtypes.float8_e5m2, 14)}[fmt]
    v = np.moveaxis(np.asarray(x, np.float32).astype(ml_dtypes.bfloat16).astype(np.float64), axis, -1)
    blocks = v.reshape(v.shape[:-1] + (-1, 32))
    amax = np.abs(blocks).max(-1, keepdims=True)
    byte = np.maximum(np.where(amax > 0, np.frexp(amax)[1] - 1 + 127, 0) - down, 1)
    scale = np.exp2(byte - 127.0)
    codes = (blocks / scale).astype(np.float32).astype(dtype).astype(np.float64)
    return np.moveaxis((codes * scale).reshape(v.shape), -1, axis)


WIDE = False


def mx_kscale(k):
    if not WIDE:
        return np.ones(k)
    levels = np.array([10, -10, 5, -5, 0])
    if k % 512:
        return np.exp2(np.random.permutation(np.resize(levels, k // 32))).repeat(32)
    a = np.empty((k // 512, 16))
    for p in range(k // 512):
        a[p, :8] = np.random.permutation(np.resize(levels, 8))
        for g in range(8):
            far = levels[np.abs(levels - a[p, g]) >= 10]
            a[p, g + 8] = far[np.random.randint(len(far))]
    return np.exp2(a.ravel()).repeat(32)


def f64(x):
    return np.asarray(x).astype(np.float64)


def striped(idx):
    return np.tile(idx.reshape(-1, 16).T, (8, 1)).astype(np.uint16)


def unstriped(offs):
    return offs[:16].T.reshape(-1).astype(np.int64)


def striped8(idx):
    return np.concatenate([x.reshape(-1, 16).T for x in idx]).astype(np.uint16)


def runs(offs, k):
    lists = np.stack([offs[16 * r : 16 * r + 16].T.reshape(-1) for r in range(8)]).astype(np.int64)
    return lists[np.arange(k) % 512 // 64]


def pack_weight(w):
    k, n = w.shape
    w = f64(np.asarray(w, np.float32).astype(ml_dtypes.bfloat16)).reshape(k // 32, 32, n)
    amax = np.abs(w).max(1)
    byte = np.clip(np.where(amax > 0, np.frexp(amax)[1] - 1 + 127 - 7, 1), 1, 254)
    scaled = (w * np.exp2(127.0 - byte)[:, None, :]).reshape(k, n).astype(np.float32)
    words = np.ascontiguousarray(scaled.reshape(k // 512, 128, 4, n).transpose(0, 1, 3, 2)).astype(ml_dtypes.float8_e4m3fn).view(np.uint8)
    return words, np.ascontiguousarray(byte.astype(np.uint8).reshape(k // 512, 16, n))


def unpack_weight(words, scales):
    g, p, n, _ = words.shape
    vals = np.ascontiguousarray(words).view(ml_dtypes.float8_e4m3fn).astype(np.float64) * np.repeat(np.exp2(scales.astype(np.float64) - 127.0), 8, axis=1)[..., None]
    return vals.transpose(0, 1, 3, 2).reshape(g * 512, n)


E2M1 = np.array([0.0, 0.5, 1.0, 1.5, 2.0, 3.0, 4.0, 6.0, -0.0, -0.5, -1.0, -1.5, -2.0, -3.0, -4.0, -6.0])


def pack_fp4(w):
    k, n = w.shape
    w = f64(np.asarray(w, np.float32).astype(ml_dtypes.bfloat16)).reshape(k // 32, 32, n)
    amax = np.abs(w).max(1)
    mant, ex = np.frexp(amax / 6.0)
    byte = np.clip(np.where(amax > 0, np.where(mant > 0.5, ex, ex - 1) + 127, 1), 1, 254)
    scaled = (w * np.exp2(127.0 - byte)[:, None, :]).reshape(k, n).astype(np.float32)
    c = np.ascontiguousarray(scaled.reshape(k // 512, 128, 4, n).transpose(0, 1, 3, 2)).astype(ml_dtypes.float4_e2m1fn).view(np.uint8) & 0xF
    words = (c[..., 0::2] | (c[..., 1::2] << 4)).reshape(k // 512, 128, 2 * n)
    return np.ascontiguousarray(words), np.ascontiguousarray(byte.astype(np.uint8).reshape(k // 512, 16, n))


def unpack_fp4(words, scales):
    g, _, n = scales.shape
    words = np.ascontiguousarray(words).reshape(g, 128, n, 2)
    nib = np.empty((g, 128, n, 4), np.uint8)
    nib[..., 0::2] = words & 0xF
    nib[..., 1::2] = words >> 4
    vals = E2M1[nib] * np.repeat(np.exp2(scales.astype(np.float64) - 127.0), 8, axis=1)[..., None]
    return vals.transpose(0, 1, 3, 2).reshape(g * 512, n)


def planes(y):
    n, m = y.shape
    v = y.astype(np.float32).astype(ml_dtypes.bfloat16).astype(np.float64).reshape(n // 32, 32, m)
    top = np.abs(v).max(1)
    byte = np.clip(np.where(top > 0, np.frexp(top)[1] - 1 + 127 - 7, 1), 1, 254)
    codes = (v * np.exp2(127.0 - byte)[:, None, :]).reshape(n, m).astype(np.float32).astype(ml_dtypes.float8_e4m3fn).view(np.uint8)
    words = codes.reshape(n // 512, 128, 4, m).transpose(0, 1, 3, 2)
    return np.ascontiguousarray(words), np.ascontiguousarray(byte.astype(np.uint8).reshape(n // 512, 16, m))


K, T, S, N, H = 512, 2048, 512, 512, 512


def setup_inputs():
    n = np.random.standard_normal
    s = mx_kscale(K)[:, None]
    u = mx_kscale(H)
    packed_xT = pack_weight(n((K, T)) * s)
    packed_w1 = pack_fp4(n((K, H)) / np.sqrt(K) / s)
    packed_w2 = pack_fp4(n((H, N)) / np.sqrt(H) / u[:, None])
    packed_w3 = pack_fp4(n((K, N)) / np.sqrt(K) / s)
    return {
        "x_words": packed_xT[0],
        "x_scales": packed_xT[1],
        "w1_words": packed_w1[0],
        "w1_scales": packed_w1[1],
        "gn": (np.random.uniform(0.5, 1.5, (H, 1)) * u[:, None]).astype(np.float32),
        "w2_words": packed_w2[0],
        "w2_scales": packed_w2[1],
        "w3_words": packed_w3[0],
        "w3_scales": packed_w3[1],
        "offs": striped(np.random.permutation(T)[:S]),
        "n1": striped8(np.stack([np.random.permutation(S) for _ in range(8)])),
        "n2": striped8(np.stack([np.random.permutation(S) for _ in range(8)])),
        "two": striped(np.random.permutation(T)[:S]),
        "n3": striped8(np.stack([np.random.permutation(S) for _ in range(8)])),
        "n4": striped8(np.stack([np.random.permutation(S) for _ in range(8)])),
    }


def reference(x_words, x_scales, w1_words, w1_scales, gn, w2_words, w2_scales, w3_words, w3_scales, offs, n1, n2, two, n3, n4):
    xq = unpack_weight(x_words, x_scales)[:, unstriped(offs)]
    y = unpack_fp4(w1_words, w1_scales).T @ xq
    ex = np.exp(y)
    z = f64(gn) * (np.log(ex + ex[np.arange(H)[:, None], runs(n1, H)]) - (y[np.arange(H)[:, None], runs(n2, H)]))
    h = unpack_fp4(w2_words, w2_scales).T @ mxq(z, 0, "e4m3")
    x_two = unpack_weight(x_words, x_scales)[:, unstriped(two)]
    d = unpack_fp4(w3_words, w3_scales).T @ x_two
    out_0 = 0.75 * (h * (d[np.arange(N)[:, None], runs(n4, N)]) - ((h[np.arange(N)[:, None], runs(n3, N)]) * d))
    return (out_0,) + planes(out_0)

from contextlib import ExitStack

import concourse.mybir as mybir

K, T, S, N, H = 512, 2048, 512, 512, 512
FLOPS = 3 * 2 * 512 * 512 * 512

F32 = mybir.dt.float32
BF16 = mybir.dt.bfloat16
I32 = mybir.dt.int32
U32 = mybir.dt.uint32
U16 = mybir.dt.uint16
U8 = mybir.dt.uint8
FP8X4 = mybir.dt.float8_e4m3fn_x4
FP4X4 = mybir.dt.float4_e2m1fn_x4
ACT = mybir.ActivationFunctionType
ALU = mybir.AluOpType

P = 128
PACK = 4
HALF = S // 2
QUARTER = S // 4
OUT_CHUNKS = ((0, 256), (256, 384), (384, 512))


def tile_picked_latecrossblse_none_po_kernel(
    tc, x_words, x_scales, w1_words, w1_scales, gn, w2_words, w2_scales, w3_words, w3_scales,
    offs, n1, n2, two, n3, n4, out_0, out_1, out_2,
):
    nc = tc.nc

    with ExitStack() as ctx:
        keep = ctx.enter_context(tc.tile_pool(name="keep", bufs=1))
        psum = ctx.enter_context(tc.psum_pool(name="psum", bufs=1))

        def sb(name, shape, dtype):
            return keep.tile(shape, dtype, name=name, align_bytes=64)

        def load_list(name, src):
            tile = keep.tile([P, S // 16], U16, name=name)
            nc.sync.dma_start(tile[:], src)
            return tile

        def entries(tile, cols):
            return tile[:, cols.start // 16 : cols.stop // 16]

        def load_scale_rows(queues, tile, src):
            for q in range(4):
                queues[q].dma_start(out=tile[32 * q : 32 * q + 4, :].bitcast(I32), in_=src[0, 4 * q : 4 * q + 4, :].bitcast(I32))

        xs = sb("xs", [P, T], U8)
        nc.vector.memset(xs[:].bitcast(I32), 0)
        ws_raw = sb("ws_raw", [P, H], U8)
        nc.vector.memset(ws_raw[:].bitcast(I32), 0)
        ww_raw = sb("ww_raw", [P, 2 * H], U8)
        ws_raw3 = sb("ws_raw3", [P, H], U8)
        nc.vector.memset(ws_raw3[:].bitcast(I32), 0)
        ww_raw3 = sb("ww_raw3", [P, 2 * H], U8)

        def load_words(raw, words):
            nc.sync.dma_start(out=raw[:].bitcast(I32), in_=words[0].bitcast(I32))

        def deal_words(w, raw):
            words = sb(f"ww{w}", [P, 2 * H], U8)
            nc.vector.tensor_copy(
                out=words[:].rearrange("p (t m b) -> p t m b", t=PACK, b=2),
                in_=raw[:].rearrange("p (m t b) -> p t m b", t=PACK, b=2),
            )
            return words

        def deal_scales(w, raw):
            scales = sb(f"ws{w}", [P, H], U8)
            nc.vector.tensor_copy(
                out=scales[:].rearrange("p (t m) -> p t m", t=PACK),
                in_=raw[:].rearrange("p (m t) -> p t m", t=PACK),
            )
            return scales

        def pick_scales(name, offsets):
            scales = sb(name, [P, S], U8)
            nc.vector.tensor_copy(out=scales[:], in_=xs[:].indirect(offsets[:]))
            return scales

        def pick_words(name, offsets):
            words = sb(name, [P, S], I32)
            nc.vector.tensor_copy(out=words[:].bitcast(U32), in_=xw[:].bitcast(U32).indirect(offsets[:]))
            return words

        def product(out, weight, t, moving, cols):
            nc.tensor.matmul_mx(
                out=out,
                lhsT=weight[0][:, 2 * P * t : 2 * P * (t + 1)].bitcast(FP4X4),
                lhsT_scale=weight[1][:, P * t : P * (t + 1)],
                rhs=moving[0][:, cols].bitcast(FP8X4),
                rhs_scale=moving[1][:, cols],
                start=True,
                stop=True,
            )

        offs_t = load_list("offs_t", offs)
        load_words(ww_raw, w1_words)
        xw = sb("xw", [P, T], I32)
        nc.sync.dma_start(out=xw[:], in_=x_words[0].rearrange("p n t -> p (n t)").bitcast(I32))
        load_scale_rows([nc.scalar] * 4, xs, x_scales)
        load_scale_rows([nc.sync, nc.sync, nc.sync, nc.gpsimd], ws_raw, w1_scales)
        two_t = load_list("two_t", two)
        load_words(ww_raw3, w3_words)
        load_scale_rows([nc.sync] * 4, ws_raw3, w3_scales)
        n1_t = load_list("n1_t", n1)
        n2_t = load_list("n2_t", n2)
        n4_t = load_list("n4_t", n4)
        n3_t = load_list("n3_t", n3)
        gn_t = sb("gn_t", [P, PACK], F32)
        nc.sync.dma_start(out=gn_t[:], in_=gn.rearrange("(p t) o -> p (t o)", t=PACK))

        whole = slice(0, S)
        w1w = deal_words(1, ww_raw)
        load_words(ww_raw, w2_words)
        one_s = pick_scales("one_s", offs_t)
        one_w = pick_words("one_w", offs_t)
        w1 = (w1w, deal_scales(1, ws_raw))
        load_scale_rows([nc.sync] * 4, ws_raw, w2_scales)
        y_bank = [psum.tile([P, S], F32, name=f"bank_a{t}") for t in range(PACK)]
        for t in range(PACK):
            product(y_bank[t][:], w1, t, (one_w, one_s), whole)
        two_s = pick_scales("two_s", two_t)

        ratio = sb("ratio", [P, PACK, S], F32)
        d = [sb(f"d{t}", [P, S], F32) for t in range(PACK)]
        dg = sb("dg", [P, PACK, S], F32)
        pair = [sb(f"pair{t}", [P, 2 * S], F32) for t in range(PACK)]
        ex1 = [sb(f"ex1_{t}", [P, S], F32) for t in range(PACK)]
        en2 = [sb(f"en2_{t}", [P, S], F32) for t in range(PACK)]
        both = [sb(f"both{t}", [P, S], F32) for t in range(PACK)]

        def scalar_tile(t):
            nc.scalar.activation(out=pair[t][:, S:], in_=y_bank[t][:], func=ACT.Exp)
            nc.scalar.activation(out=ex1[t][:], in_=pair[t][:].indirect(n1_t[:]), func=ACT.Exp)
            nc.scalar.activation(out=en2[t][:], in_=pair[t][:].indirect(n2_t[:]), func=ACT.Exp, scale=-1.0)

        def combine(engine, t):
            engine.tensor_tensor(out=both[t][:], in0=pair[t][:, S:], in1=ex1[t][:], op=ALU.add)
            engine.tensor_tensor(out=ratio[:, t, :], in0=both[t][:], in1=en2[t][:], op=ALU.mult)

        def fetch_d(t):
            for hf in range(2):
                cols = slice(hf * HALF, (hf + 1) * HALF)
                nc.vector.tensor_copy(out=dg[:, t, cols], in_=d[t][:].indirect(entries(n4_t, cols)))

        def empty_d(t):
            nc.scalar.activation(out=d[t][:], in_=d_bank[t][:], func=ACT.Copy, scale=0.75)

        def empty_d_v(t):
            nc.vector.tensor_scalar(out=d[t][:], in0=d_bank[t][:], scalar1=0.75, scalar2=None, op0=ALU.mult)

        def vector_tile_front(t):
            nc.scalar.activation(out=ex1[t][:], in_=y_bank[t][:], func=ACT.Exp)
            nc.scalar.activation(out=pair[t][:, :S], in_=y_bank[t][:], func=ACT.Exp)
            nc.scalar.activation(out=en2[t][:], in_=y_bank[t][:], func=ACT.Exp, scale=-1.0)

        def vector_tile_back(t):
            for hf in range(2):
                cols = slice(hf * HALF, (hf + 1) * HALF)
                nc.vector.tensor_tensor(out=both[t][:, cols], in0=ex1[t][:].indirect(entries(n1_t, cols)), in1=pair[t][:, cols], op=ALU.add)
            for hf in range(2):
                cols = slice(hf * HALF, (hf + 1) * HALF)
                nc.vector.tensor_tensor(out=ratio[:, t, cols], in0=en2[t][:].indirect(entries(n2_t, cols)), in1=both[t][:, cols], op=ALU.mult)

        def plain_tile_front(t):
            nc.scalar.activation(out=ex1[t][:], in_=y_bank[t][:], func=ACT.Exp)
            nc.scalar.activation(out=en2[t][:], in_=y_bank[t][:], func=ACT.Exp, scale=-1.0)

        def plain_tile_back(t):
            for hf in range(2):
                cols = slice(hf * HALF, (hf + 1) * HALF)
                nc.vector.tensor_copy(out=pair[t][:, cols], in_=ex1[t][:].indirect(entries(n1_t, cols)))
            for hf in range(2):
                cols = slice(hf * HALF, (hf + 1) * HALF)
                nc.vector.tensor_copy(out=pair[t][:, S + hf * HALF : S + (hf + 1) * HALF], in_=en2[t][:].indirect(entries(n2_t, cols)))
            nc.gpsimd.tensor_tensor(out=both[t][:], in0=pair[t][:, :S], in1=ex1[t][:], op=ALU.add)
            nc.gpsimd.tensor_tensor(out=ratio[:, t, :], in0=both[t][:], in1=pair[t][:, S:], op=ALU.mult)

        def empty_y(t):
            nc.vector.tensor_copy(out=pair[t][:, :S], in_=y_bank[t][:])

        def second_stream():
            two_w = pick_words("two_w", two_t)
            w3 = (deal_words(3, ww_raw3), deal_scales(3, ws_raw3))
            for t in range(PACK):
                product(d_bank[t][:], w3, t, (two_w, two_s), whole)

        d_bank = [psum.tile([P, S], F32, name=f"bank_b{t}") for t in range(PACK)]
        vector_tile_front(0)
        for t in (1, 2, 3):
            empty_y(t)
        scalar_tile(1)
        second_stream()
        vector_tile_back(0)
        scalar_tile(2)
        empty_d(0)
        empty_d(1)
        empty_d_v(2)
        empty_d_v(3)
        combine(nc.vector, 1)
        fetch_d(2)
        fetch_d(3)
        scalar_tile(3)
        combine(nc.vector, 2)
        w2 = (deal_words(2, ww_raw), deal_scales(2, ws_raw))
        fetch_d(0)
        combine(nc.vector, 3)
        fetch_d(1)

        logs = sb("logs", [P, PACK, S], F32)
        z_bf = sb("z_bf", [P, S * PACK], BF16)
        z_w = sb("z_w", [P, S], I32)
        z_s = sb("z_s", [P, S], U8)
        h = [sb(f"h{t}", [P, S], F32) for t in range(PACK)]
        direct = sb("direct", [P, PACK, S], F32)
        h_bank = [psum.tile([P, PACK, QUARTER], F32, name=f"bank_a{c}") for c in range(4)]
        quarters = [slice(c * QUARTER, (c + 1) * QUARTER) for c in range(4)]
        for cols in quarters:
            nc.scalar.activation(out=logs[:, :, cols], in_=ratio[:, :, cols], func=ACT.Ln)

        def scale_z(c):
            cols = quarters[c]
            nc.vector.tensor_tensor(
                out=z_bf[:, cols.start * PACK : cols.stop * PACK].rearrange("p (c i t) -> p c t i", i=4, t=PACK),
                in0=logs[:, :, cols].rearrange("p t (c i) -> p c t i", i=4),
                in1=gn_t[:].unsqueeze(1).unsqueeze(3).to_broadcast([P, QUARTER // 4, PACK, 4]),
                op=ALU.mult,
            )

        def multiply_z(c):
            cols = quarters[c]
            nc.vector.quantize_mx(out=z_w[:, cols].bitcast(FP8X4), scales=z_s[:, cols], in_=z_bf[:, cols.start * PACK : cols.stop * PACK])
            for t in range(PACK):
                product(h_bank[c][:, t, :], w2, t, (z_w, z_s), cols)
            for t in range(PACK):
                nc.scalar.copy(out=h[t][:, cols], in_=h_bank[c][:, t, :])

        def direct_term(c):
            cols = quarters[c]
            nc.vector.tensor_tensor(out=direct[:, :, cols], in0=h_bank[c][:], in1=dg[:, :, cols], op=ALU.mult)

        scale_z(0)
        for c in range(1, 4):
            scale_z(c)
            multiply_z(c - 1)
        direct_term(0)
        multiply_z(3)
        for c in range(1, 4):
            direct_term(c)

        crossed = sb("crossed", [P, PACK, S], F32)
        res = sb("res", [P, PACK, S], F32)
        res_bf = sb("res_bf", [P, S * PACK], BF16)
        res_w = sb("res_w", [P, S], I32)
        res_s = sb("res_s", [P, S], U8)
        out_rows = out_0.rearrange("(p t) j -> p t j", t=PACK)
        out_words = out_1[0].rearrange("p n t -> p (n t)").bitcast(I32)

        def finish(cols):
            nc.vector.quantize_mx(out=res_w[:, cols].bitcast(FP8X4), scales=res_s[:, cols], in_=res_bf[:, cols.start * PACK : cols.stop * PACK])
            nc.sync.dma_start(out=out_words[:, cols], in_=res_w[:, cols])

        chunks = [slice(a, b) for a, b in OUT_CHUNKS]
        for n, cols in enumerate(chunks):
            for t in range(PACK):
                nc.vector.tensor_tensor(out=crossed[:, t, cols], in0=h[t][:].indirect(entries(n3_t, cols)), in1=d[t][:, cols], op=ALU.mult)
            if n:
                finish(chunks[n - 1])
            nc.vector.tensor_tensor(out=res[:, :, cols], in0=direct[:, :, cols], in1=crossed[:, :, cols], op=ALU.subtract)
            nc.sync.dma_start(out=out_rows[:, :, cols], in_=res[:, :, cols])
            rounded = res_bf[:, cols.start * PACK : cols.stop * PACK].rearrange("p (c i t) -> p c t i", i=4, t=PACK)
            exact = res[:, :, cols].rearrange("p t (c i) -> p c t i", i=4)
            if n < len(chunks) - 1:
                nc.scalar.copy(out=rounded, in_=exact)
            else:
                nc.vector.tensor_copy(out=rounded, in_=exact)
        finish(chunks[-1])
        for q in range(4):
            queue = nc.sync if q == 3 else nc.scalar
            queue.dma_start(out=out_2[0, 4 * q : 4 * q + 4, :].bitcast(I32), in_=res_s[32 * q : 32 * q + 4, :].bitcast(I32))
